import numpy as np
import ml_dtypes


def mxq(x, axis, fmt="e4m3"):
    dtype, down = {"e4m3": (ml_dtypes.float8_e4m3fn, 7), "e5m2": (ml_dtypes.float8_e5m2, 14)}[fmt]
    v = np.moveaxis(np.asarray(x, np.float32).astype(ml_dtypes.bfloat16).astype(np.float64), axis, -1)
    blocks = v.reshape(v.shape[:-1] + (-1, 32))
    amax = np.abs(blocks).max(-1, keepdims=True)
    byte = np.maximum(np.where(amax > 0, np.frexp(amax)[1] - 1 + 127, 0) - down, 1)
    scale = np.exp2(byte - 127.0)
    codes = (blocks / scale).astype(np.float32).astype(dtype).astype(np.float64)
    return np.moveaxis((codes * scale).reshape(v.shape), -1, axis)


WIDE = False


def mx_kscale(k):
    if not WIDE:
        return np.ones(k)
    levels = np.array([10, -10, 5, -5, 0])
    if k % 512:
        return np.exp2(np.random.permutation(np.resize(levels, k // 32))).repeat(32)
    a = np.empty((k // 512, 16))
    for p in range(k // 512):
        a[p, :8] = np.random.permutation(np.resize(levels, 8))
        for g in range(8):
            far = levels[np.abs(levels - a[p, g]) >= 10]
            a[p, g + 8] = far[np.random.randint(len(far))]
    return np.exp2(a.ravel()).repeat(32)


def f64(x):
    return np.asarray(x).astype(np.float64)


def striped(idx):
    return np.tile(idx.reshape(-1, 16).T, (8, 1)).astype(np.uint16)


def unstriped(offs):
    return offs[:16].T.reshape(-1).astype(np.int64)


def relu(v):
    return np.maximum(v, 0.0)


K, T, E, C, N = 1536, 768, 4, 128, 512


def by_expert(wq, xq):
    return np.concatenate([wq[e].T @ xq[:, e * C:(e + 1) * C] for e in range(E)], axis=1)


def setup_inputs():
    n = np.random.standard_normal
    s = mx_kscale(K)[:, None]
    return {
        "xT": (n((K, T)) * s).astype(np.float32),
        "w": (n((E, K, N)) / np.sqrt(K) / s[None]).astype(np.float32),
        "b": (0.3 * n((N, E))).astype(np.float32),
        "gate": np.tile(np.random.uniform(0.2, 1.0, E * C), (N, 1)).astype(np.float32),
        "offs": striped(np.random.permutation(T)[:E * C]),
    }


def reference(xT, w, b, gate, offs):
    idx = unstriped(offs)
    xq = mxq(f64(xT)[:, idx], 0, "e4m3")
    y = by_expert(mxq(f64(w), 1, "e4m3"), xq)
    y = relu(y + np.repeat(f64(b), C, axis=1))
    out = np.zeros((N, T))
    out[:, idx] = f64(gate) * y
    return out

@@ -1,0 +1,135 @@
+from contextlib import ExitStack
+
+import concourse.mybir as mybir
+
+K, T, E, C, N = 1536, 768, 4, 128, 512
+P = 128
+PACK = 4
+A = K // (P * PACK)
+S = E * C
+M = N // P
+
+FLOPS = 2 * K * N * S
+BYTES = 4 * (K * T + E * K * N + N * E + P * S + N * T) + 2 * P * (S // 16)
+
+F32 = mybir.dt.float32
+BF16 = mybir.dt.bfloat16
+U32 = mybir.dt.uint32
+U16 = mybir.dt.uint16
+U8 = mybir.dt.uint8
+FP8X4 = mybir.dt.float8_e4m3fn_x4
+RELU = mybir.ActivationFunctionType.Relu
+MULT = mybir.AluOpType.mult
+
+
+def lay_side_by_side(copy, grouped, raw, lo, hi):
+    copy(
+        out=grouped[:, lo:hi, :].rearrange("p (c i) t -> p c t i", i=4),
+        in_=raw[:, :, lo:hi].rearrange("p t (c i) -> p c t i", i=4),
+    )
+
+
+def tile_routed_moe_kernel(tc, xT, w, b, gate, offs, out):
+    nc = tc.nc
+    with ExitStack() as ctx:
+        keep = ctx.enter_context(tc.tile_pool(name="keep", bufs=1))
+        xstage = ctx.enter_context(tc.tile_pool(name="xstage", bufs=2))
+        wstage = ctx.enter_context(tc.tile_pool(name="wstage", bufs=3))
+        ypool = ctx.enter_context(tc.tile_pool(name="ypool", bufs=6))
+        psum = ctx.enter_context(tc.psum_pool(name="psum", bufs=2))
+
+        x_rows = xT.rearrange("(a p t) n -> a p t n", p=P, t=PACK)
+        w_rows = w.rearrange("e (a p t) n -> e a p t n", p=P, t=PACK)
+
+        offsets = keep.tile([P, S // 16], U16, name="offsets")
+        x_raw = [keep.tile([P, PACK, T], F32, name=f"x_raw{a}") for a in range(A)]
+        x_codes = [keep.tile([P, T], U32, name=f"x_codes{a}", align_bytes=64) for a in range(A)]
+        x_scales = keep.tile([P, T], U8, name="x_scales", align_bytes=64)
+        s_codes = [keep.tile([P, S], U32, name=f"s_codes{a}", align_bytes=64) for a in range(A)]
+        s_scales = keep.tile([P, S], U8, name="s_scales", align_bytes=64)
+        bias = keep.tile([P, M, E], F32, name="bias")
+        gates = keep.tile([P, S], F32, name="gates")
+        windows = [keep.tile([P, T], F32, name=f"window{m}") for m in range(M)]
+
+        w_raw = {}
+        w_codes = {}
+        w_scales = {}
+        for e in range(E):
+            for a in range(A):
+                w_raw[e, a] = keep.tile([P, PACK, N], F32, name=f"w_raw{e}_{a}")
+                w_codes[e, a] = keep.tile([P, N], U32, name=f"w_codes{e}_{a}", align_bytes=64)
+                w_scales[e, a] = keep.tile([P, N], U8, name=f"w_scales{e}_{a}", align_bytes=64)
+
+        nc.gpsimd.memset(x_scales[:], 0)
+
+        nc.sync.dma_start(x_raw[0][:, :, 0:256], x_rows[0, :, :, 0:256])
+        nc.sync.dma_start(x_raw[0][:, :, 256:T], x_rows[0, :, :, 256:T])
+        nc.sync.dma_start(offsets[:], offs)
+        nc.sync.dma_start(x_raw[1][:], x_rows[1])
+        nc.sync.dma_start(x_raw[2][:], x_rows[2])
+        nc.sync.dma_start(bias[:], b.rearrange("(m p) e -> p m e", p=P))
+        for e in range(E):
+            for a in range(A):
+                if (e, a) == (E - 1, A - 1):
+                    for lo, hi in ((0, 256), (256, 512)):
+                        nc.sync.dma_start(w_raw[e, a][:, :, lo:hi], w_rows[e, a, :, :, lo:hi])
+                else:
+                    nc.sync.dma_start(w_raw[e, a][:], w_rows[e, a])
+                if (e, a) == (0, 0):
+                    nc.sync.dma_start(gates[:], gate[0:P, :])
+
+        for m in range(M):
+            nc.vector.memset(windows[m][:], 0.0)
+
+        for a in range(A):
+            grouped = xstage.tile([P, T, PACK], BF16, name="x_grouped", align_bytes=64)
+            for lo, mid, hi in ((0, 192, 256), (256, 640, 768)):
+                lay_side_by_side(nc.scalar.copy, grouped, x_raw[a], lo, mid)
+                lay_side_by_side(nc.vector.tensor_copy, grouped, x_raw[a], mid, hi)
+            for lo, hi in ((0, 256), (256, 768)):
+                nc.vector.quantize_mx(
+                    out=x_codes[a][:, lo:hi].bitcast(FP8X4),
+                    scales=x_scales[4 * a : P, lo:hi],
+                    in_=grouped[:, lo:hi, :].rearrange("p n t -> p (n t)"),
+                )
+            nc.vector.tensor_copy(s_codes[a][:], x_codes[a][:].indirect(offsets[:]))
+        nc.vector.tensor_copy(s_scales[:], x_scales[:].indirect(offsets[:]))
+
+        for e in range(E):
+            acc = [psum.tile([P, C], F32, name=f"acc{m}") for m in range(M)]
+            slots = slice(e * C, (e + 1) * C)
+            for a in range(A):
+                grouped = wstage.tile([P, N, PACK], BF16, name="w_grouped", align_bytes=64)
+                pieces = ((0, 384, 512),)
+                if (e, a) == (E - 1, A - 1):
+                    pieces = ((0, 160, 256), (256, 384, 512))
+                for lo, mid, hi in pieces:
+                    lay_side_by_side(nc.scalar.copy, grouped, w_raw[e, a], lo, mid)
+                    lay_side_by_side(nc.vector.tensor_copy, grouped, w_raw[e, a], mid, hi)
+                    nc.vector.quantize_mx(
+                        out=w_codes[e, a][:, lo:hi].bitcast(FP8X4),
+                        scales=w_scales[e, a][:, lo:hi],
+                        in_=grouped[:, lo:hi, :].rearrange("p n t -> p (n t)"),
+                    )
+                    for m in range(lo // P, hi // P):
+                        cols = slice(m * P, (m + 1) * P)
+                        nc.tensor.matmul_mx(
+                            out=acc[m][:],
+                            lhsT=w_codes[e, a][:, cols].bitcast(FP8X4),
+                            lhsT_scale=w_scales[e, a][:, cols],
+                            rhs=s_codes[a][:, slots].bitcast(FP8X4),
+                            rhs_scale=s_scales[4 * a : P, slots],
+                            start=(a == 0),
+                            stop=(a == A - 1),
+                        )
+            for m in range(M):
+                y = ypool.tile([P, C], F32, name="y")
+                nc.scalar.activation(out=y[:], in_=acc[m][:], func=RELU, bias=bias[:, m, e : e + 1], scale=1.0)
+                nc.vector.tensor_tensor(
+                    windows[m][:].indirect(offsets[:, e * C // 16 : (e + 1) * C // 16]),
+                    y[:],
+                    gates[:, slots],
+                    MULT,
+                )
+                if e == E - 1:
+                    nc.sync.dma_start(out[m * P : (m + 1) * P, :], windows[m][:])

@@ -19,6 +19,9 @@ U16 = mybir.dt.uint16
 U8 = mybir.dt.uint8
 FP8X4 = mybir.dt.float8_e4m3fn_x4
 RELU = mybir.ActivationFunctionType.Relu
+X_PIECES = (((0, 48, 128), (128, 176, 256), (256, 512, 768)), ((0, 384, 768),))
+W_PIECES = {(e, a): (((0, 160, 256), (256, 416, 512)) if a == 2 else ((0, 448, 512),)) for e in range(E) for a in range(A)}
+PUT_AFTER = (4, 4)
 MULT = mybir.AluOpType.mult
 
 
@@ -35,7 +38,7 @@ def tile_routed_moe_kernel(tc, xT, w, b, gate, offs, out):
         keep = ctx.enter_context(tc.tile_pool(name="keep", bufs=1))
         xstage = ctx.enter_context(tc.tile_pool(name="xstage", bufs=2))
         wstage = ctx.enter_context(tc.tile_pool(name="wstage", bufs=3))
-        ypool = ctx.enter_context(tc.tile_pool(name="ypool", bufs=6))
+        ypool = ctx.enter_context(tc.tile_pool(name="ypool", bufs=8))
         psum = ctx.enter_context(tc.psum_pool(name="psum", bufs=2))
 
         x_rows = xT.rearrange("(a p t) n -> a p t n", p=P, t=PACK)
@@ -61,8 +64,12 @@ def tile_routed_moe_kernel(tc, xT, w, b, gate, offs, out):
                 w_scales[e, a] = keep.tile([P, N], U8, name=f"w_scales{e}_{a}", align_bytes=64)
 
         nc.gpsimd.memset(x_scales[:], 0)
+        warm = keep.tile([P, 2], F32, name="warm")
+        nc.vector.memset(warm[:], 0.0)
+        nc.scalar.activation(out=warm[:, 1:2], in_=warm[:, 0:1], func=RELU)
 
-        nc.sync.dma_start(x_raw[0][:, :, 0:256], x_rows[0, :, :, 0:256])
+        for lo, hi in ((0, 128), (128, 256)):
+            nc.sync.dma_start(x_raw[0][:, :, lo:hi], x_rows[0, :, :, lo:hi])
         nc.sync.dma_start(x_raw[0][:, :, 256:T], x_rows[0, :, :, 256:T])
         nc.sync.dma_start(offsets[:], offs)
         nc.sync.dma_start(x_raw[1][:], x_rows[1])
@@ -83,7 +90,8 @@ def tile_routed_moe_kernel(tc, xT, w, b, gate, offs, out):
 
         for a in range(A):
             grouped = xstage.tile([P, T, PACK], BF16, name="x_grouped", align_bytes=64)
-            for lo, mid, hi in ((0, 192, 256), (256, 640, 768)):
+            pieces = X_PIECES[min(a, 1)]
+            for lo, mid, hi in pieces:
                 lay_side_by_side(nc.scalar.copy, grouped, x_raw[a], lo, mid)
                 lay_side_by_side(nc.vector.tensor_copy, grouped, x_raw[a], mid, hi)
             for lo, hi in ((0, 256), (256, 768)):
@@ -95,17 +103,27 @@ def tile_routed_moe_kernel(tc, xT, w, b, gate, offs, out):
             nc.vector.tensor_copy(s_codes[a][:], x_codes[a][:].indirect(offsets[:]))
         nc.vector.tensor_copy(s_scales[:], x_scales[:].indirect(offsets[:]))
 
+        def put_back(e, m, y):
+            nc.vector.tensor_tensor(
+                windows[m][:].indirect(offsets[:, e * C // 16 : (e + 1) * C // 16]),
+                y[:],
+                gates[:, e * C : (e + 1) * C],
+                MULT,
+            )
+            if e == E - 1:
+                nc.sync.dma_start(out[m * P : (m + 1) * P, :], windows[m][:])
+
+        waiting = []
         for e in range(E):
             acc = [psum.tile([P, C], F32, name=f"acc{m}") for m in range(M)]
             slots = slice(e * C, (e + 1) * C)
             for a in range(A):
                 grouped = wstage.tile([P, N, PACK], BF16, name="w_grouped", align_bytes=64)
-                pieces = ((0, 384, 512),)
-                if (e, a) == (E - 1, A - 1):
-                    pieces = ((0, 160, 256), (256, 384, 512))
-                for lo, mid, hi in pieces:
-                    lay_side_by_side(nc.scalar.copy, grouped, w_raw[e, a], lo, mid)
-                    lay_side_by_side(nc.vector.tensor_copy, grouped, w_raw[e, a], mid, hi)
+                for lo, mid, hi in W_PIECES[e, a]:
+                    if mid > lo:
+                        lay_side_by_side(nc.scalar.copy, grouped, w_raw[e, a], lo, mid)
+                    if hi > mid:
+                        lay_side_by_side(nc.vector.tensor_copy, grouped, w_raw[e, a], mid, hi)
                     nc.vector.quantize_mx(
                         out=w_codes[e, a][:, lo:hi].bitcast(FP8X4),
                         scales=w_scales[e, a][:, lo:hi],
@@ -122,14 +140,11 @@ def tile_routed_moe_kernel(tc, xT, w, b, gate, offs, out):
                             start=(a == 0),
                             stop=(a == A - 1),
                         )
-            for m in range(M):
-                y = ypool.tile([P, C], F32, name="y")
-                nc.scalar.activation(out=y[:], in_=acc[m][:], func=RELU, bias=bias[:, m, e : e + 1], scale=1.0)
-                nc.vector.tensor_tensor(
-                    windows[m][:].indirect(offsets[:, e * C // 16 : (e + 1) * C // 16]),
-                    y[:],
-                    gates[:, slots],
-                    MULT,
-                )
-                if e == E - 1:
-                    nc.sync.dma_start(out[m * P : (m + 1) * P, :], windows[m][:])
+                        if a == A - 1:
+                            y = ypool.tile([P, C], F32, name="y")
+                            nc.scalar.activation(out=y[:], in_=acc[m][:], func=RELU, bias=bias[:, m, e : e + 1], scale=1.0)
+                            waiting.append((e, m, y))
+                for job in [waiting.pop(0) for i in range(min(len(waiting), PUT_AFTER[a]))] if a < A - 1 else []:
+                    put_back(*job)
+        for job in waiting:
+            put_back(*job)

from contextlib import ExitStack

import concourse.mybir as mybir

K, T, E, C, N = 1536, 768, 4, 128, 512
P = 128
PACK = 4
A = K // (P * PACK)
S = E * C
M = N // P

FLOPS = 2 * K * N * S
BYTES = 4 * (K * T + E * K * N + N * E + P * S + N * T) + 2 * P * (S // 16)

F32 = mybir.dt.float32
BF16 = mybir.dt.bfloat16
U32 = mybir.dt.uint32
U16 = mybir.dt.uint16
U8 = mybir.dt.uint8
FP8X4 = mybir.dt.float8_e4m3fn_x4
RELU = mybir.ActivationFunctionType.Relu
X_PIECES = (((0, 48, 128), (128, 176, 256), (256, 512, 768)), ((0, 384, 768),))
W_PIECES = {(e, a): (((0, 160, 256), (256, 416, 512)) if a == 2 else ((0, 448, 512),)) for e in range(E) for a in range(A)}
PUT_AFTER = (4, 4)
MULT = mybir.AluOpType.mult


def lay_side_by_side(copy, grouped, raw, lo, hi):
    copy(
        out=grouped[:, lo:hi, :].rearrange("p (c i) t -> p c t i", i=4),
        in_=raw[:, :, lo:hi].rearrange("p t (c i) -> p c t i", i=4),
    )


def tile_routed_moe_kernel(tc, xT, w, b, gate, offs, out):
    nc = tc.nc
    with ExitStack() as ctx:
        keep = ctx.enter_context(tc.tile_pool(name="keep", bufs=1))
        xstage = ctx.enter_context(tc.tile_pool(name="xstage", bufs=2))
        wstage = ctx.enter_context(tc.tile_pool(name="wstage", bufs=3))
        ypool = ctx.enter_context(tc.tile_pool(name="ypool", bufs=8))
        psum = ctx.enter_context(tc.psum_pool(name="psum", bufs=2))

        x_rows = xT.rearrange("(a p t) n -> a p t n", p=P, t=PACK)
        w_rows = w.rearrange("e (a p t) n -> e a p t n", p=P, t=PACK)

        offsets = keep.tile([P, S // 16], U16, name="offsets")
        x_raw = [keep.tile([P, PACK, T], F32, name=f"x_raw{a}") for a in range(A)]
        x_codes = [keep.tile([P, T], U32, name=f"x_codes{a}", align_bytes=64) for a in range(A)]
        x_scales = keep.tile([P, T], U8, name="x_scales", align_bytes=64)
        s_codes = [keep.tile([P, S], U32, name=f"s_codes{a}", align_bytes=64) for a in range(A)]
        s_scales = keep.tile([P, S], U8, name="s_scales", align_bytes=64)
        bias = keep.tile([P, M, E], F32, name="bias")
        gates = keep.tile([P, S], F32, name="gates")
        windows = [keep.tile([P, T], F32, name=f"window{m}") for m in range(M)]

        w_raw = {}
        w_codes = {}
        w_scales = {}
        for e in range(E):
            for a in range(A):
                w_raw[e, a] = keep.tile([P, PACK, N], F32, name=f"w_raw{e}_{a}")
                w_codes[e, a] = keep.tile([P, N], U32, name=f"w_codes{e}_{a}", align_bytes=64)
                w_scales[e, a] = keep.tile([P, N], U8, name=f"w_scales{e}_{a}", align_bytes=64)

        nc.gpsimd.memset(x_scales[:], 0)
        warm = keep.tile([P, 2], F32, name="warm")
        nc.vector.memset(warm[:], 0.0)
        nc.scalar.activation(out=warm[:, 1:2], in_=warm[:, 0:1], func=RELU)

        for lo, hi in ((0, 128), (128, 256)):
            nc.sync.dma_start(x_raw[0][:, :, lo:hi], x_rows[0, :, :, lo:hi])
        nc.sync.dma_start(x_raw[0][:, :, 256:T], x_rows[0, :, :, 256:T])
        nc.sync.dma_start(offsets[:], offs)
        nc.sync.dma_start(x_raw[1][:], x_rows[1])
        nc.sync.dma_start(x_raw[2][:], x_rows[2])
        nc.sync.dma_start(bias[:], b.rearrange("(m p) e -> p m e", p=P))
        for e in range(E):
            for a in range(A):
                if (e, a) == (E - 1, A - 1):
                    for lo, hi in ((0, 256), (256, 512)):
                        nc.sync.dma_start(w_raw[e, a][:, :, lo:hi], w_rows[e, a, :, :, lo:hi])
                else:
                    nc.sync.dma_start(w_raw[e, a][:], w_rows[e, a])
                if (e, a) == (0, 0):
                    nc.sync.dma_start(gates[:], gate[0:P, :])

        for m in range(M):
            nc.vector.memset(windows[m][:], 0.0)

        for a in range(A):
            grouped = xstage.tile([P, T, PACK], BF16, name="x_grouped", align_bytes=64)
            pieces = X_PIECES[min(a, 1)]
            for lo, mid, hi in pieces:
                lay_side_by_side(nc.scalar.copy, grouped, x_raw[a], lo, mid)
                lay_side_by_side(nc.vector.tensor_copy, grouped, x_raw[a], mid, hi)
            for lo, hi in ((0, 256), (256, 768)):
                nc.vector.quantize_mx(
                    out=x_codes[a][:, lo:hi].bitcast(FP8X4),
                    scales=x_scales[4 * a : P, lo:hi],
                    in_=grouped[:, lo:hi, :].rearrange("p n t -> p (n t)"),
                )
            nc.vector.tensor_copy(s_codes[a][:], x_codes[a][:].indirect(offsets[:]))
        nc.vector.tensor_copy(s_scales[:], x_scales[:].indirect(offsets[:]))

        def put_back(e, m, y):
            nc.vector.tensor_tensor(
                windows[m][:].indirect(offsets[:, e * C // 16 : (e + 1) * C // 16]),
                y[:],
                gates[:, e * C : (e + 1) * C],
                MULT,
            )
            if e == E - 1:
                nc.sync.dma_start(out[m * P : (m + 1) * P, :], windows[m][:])

        waiting = []
        for e in range(E):
            acc = [psum.tile([P, C], F32, name=f"acc{m}") for m in range(M)]
            slots = slice(e * C, (e + 1) * C)
            for a in range(A):
                grouped = wstage.tile([P, N, PACK], BF16, name="w_grouped", align_bytes=64)
                for lo, mid, hi in W_PIECES[e, a]:
                    if mid > lo:
                        lay_side_by_side(nc.scalar.copy, grouped, w_raw[e, a], lo, mid)
                    if hi > mid:
                        lay_side_by_side(nc.vector.tensor_copy, grouped, w_raw[e, a], mid, hi)
                    nc.vector.quantize_mx(
                        out=w_codes[e, a][:, lo:hi].bitcast(FP8X4),
                        scales=w_scales[e, a][:, lo:hi],
                        in_=grouped[:, lo:hi, :].rearrange("p n t -> p (n t)"),
                    )
                    for m in range(lo // P, hi // P):
                        cols = slice(m * P, (m + 1) * P)
                        nc.tensor.matmul_mx(
                            out=acc[m][:],
                            lhsT=w_codes[e, a][:, cols].bitcast(FP8X4),
                            lhsT_scale=w_scales[e, a][:, cols],
                            rhs=s_codes[a][:, slots].bitcast(FP8X4),
                            rhs_scale=s_scales[4 * a : P, slots],
                            start=(a == 0),
                            stop=(a == A - 1),
                        )
                        if a == A - 1:
                            y = ypool.tile([P, C], F32, name="y")
                            nc.scalar.activation(out=y[:], in_=acc[m][:], func=RELU, bias=bias[:, m, e : e + 1], scale=1.0)
                            waiting.append((e, m, y))
                for job in [waiting.pop(0) for i in range(min(len(waiting), PUT_AFTER[a]))] if a < A - 1 else []:
                    put_back(*job)
        for job in waiting:
            put_back(*job)
